import numpy as np
import ml_dtypes


def mxq(x, axis, fmt="e4m3"):
    dtype, down = {"e4m3": (ml_dtypes.float8_e4m3fn, 7), "e5m2": (ml_dtypes.float8_e5m2, 14)}[fmt]
    v = np.moveaxis(np.asarray(x, np.float32).astype(ml_dtypes.bfloat16).astype(np.float64), axis, -1)
    blocks = v.reshape(v.shape[:-1] + (-1, 32))
    amax = np.abs(blocks).max(-1, keepdims=True)
    byte = np.maximum(np.where(amax > 0, np.frexp(amax)[1] - 1 + 127, 0) - down, 1)
    scale = np.exp2(byte - 127.0)
    codes = (blocks / scale).astype(np.float32).astype(dtype).astype(np.float64)
    return np.moveaxis((codes * scale).reshape(v.shape), -1, axis)


WIDE = False


def mx_kscale(k):
    if not WIDE:
        return np.ones(k)
    levels = np.array([10, -10, 5, -5, 0])
    if k % 512:
        return np.exp2(np.random.permutation(np.resize(levels, k // 32))).repeat(32)
    a = np.empty((k // 512, 16))
    for p in range(k // 512):
        a[p, :8] = np.random.permutation(np.resize(levels, 8))
        for g in range(8):
            far = levels[np.abs(levels - a[p, g]) >= 10]
            a[p, g + 8] = far[np.random.randint(len(far))]
    return np.exp2(a.ravel()).repeat(32)


def f64(x):
    return np.asarray(x).astype(np.float64)


def striped(idx):
    return np.tile(np.asarray(idx).reshape(-1, 16).T, (8, 1)).astype(np.uint16)


def unstriped(offs):
    return offs[:16].T.reshape(-1).astype(np.int64)


E2M1 = np.array([0.0, 0.5, 1.0, 1.5, 2.0, 3.0, 4.0, 6.0, -0.0, -0.5, -1.0, -1.5, -2.0, -3.0, -4.0, -6.0])


def pack_weight(w, fmt):
    k, n = w.shape
    w = f64(np.asarray(w, np.float32).astype(ml_dtypes.bfloat16)).reshape(k // 32, 32, n)
    amax = np.abs(w).max(1)
    if fmt == "e4m3":
        byte = np.frexp(amax)[1] - 1 + 127 - 7
    else:
        mant, ex = np.frexp(amax / 6.0)
        byte = np.where(mant > 0.5, ex, ex - 1) + 127
    byte = np.clip(np.where(amax > 0, byte, 1), 1, 254)
    scaled = (w * np.exp2(127.0 - byte)[:, None, :]).reshape(k, n).astype(np.float32)
    by_word = np.ascontiguousarray(scaled.reshape(k // 512, 128, 4, n).transpose(0, 1, 3, 2))
    if fmt == "e4m3":
        words = by_word.astype(ml_dtypes.float8_e4m3fn).view(np.uint8)
    else:
        c = by_word.astype(ml_dtypes.float4_e2m1fn).view(np.uint8) & 0xF
        words = (c[..., 0::2] | (c[..., 1::2] << 4)).reshape(k // 512, 128, 2 * n)
    return np.ascontiguousarray(words), np.ascontiguousarray(byte.astype(np.uint8).reshape(k // 512, 16, n))


def unpack_weight(words, scales, fmt):
    g, _, n = scales.shape
    words = np.ascontiguousarray(words).reshape(g, 128, n, -1)
    if fmt == "e4m3":
        vals = words.view(ml_dtypes.float8_e4m3fn).astype(np.float64)
    else:
        nib = np.empty((g, 128, n, 4), np.uint8)
        nib[..., 0::2] = words & 0xF
        nib[..., 1::2] = words >> 4
        vals = E2M1[nib]
    vals = vals * np.repeat(np.exp2(scales.astype(np.float64) - 127.0), 8, axis=1)[..., None]
    return vals.transpose(0, 1, 3, 2).reshape(g * 512, n)


def bf(x):
    return np.asarray(x, np.float32).astype(ml_dtypes.bfloat16)


def planes(Y):
    r, m = Y.shape
    b = f64(bf(Y)).reshape(r // 32, 32, m)
    amax = np.abs(b).max(1)
    byte = np.clip(np.where(amax > 0, np.frexp(amax)[1] - 1 + 127 - 7, 1), 1, 254)
    codes = (b * np.exp2(127.0 - byte)[:, None, :]).reshape(r, m).astype(np.float32).astype(ml_dtypes.float8_e4m3fn).view(np.uint8)
    words = codes.reshape(r // 512, 128, 4, m).transpose(0, 1, 3, 2)
    return np.ascontiguousarray(words), np.ascontiguousarray(byte.astype(np.uint8).reshape(r // 512, 16, m))


D, T, I, J, U, X, Z, E = 512, 2048, 512, 512, 1024, 1024, 1024, 512


def setup_inputs():
    n = np.random.standard_normal
    idx = np.random.permutation(T)[:I]
    idx2 = np.random.permutation(U)[:J]
    idx3 = np.random.permutation(X)[:I]
    idx4 = np.random.permutation(Z)[:J]
    fd = mx_kscale(D)
    fi = mx_kscale(I)
    ti = np.ones(T)
    ti[idx] = fi
    keysp = pack_weight(n((D, T)) / fd[:, None], "e2m1")
    morep = pack_weight(n((D, X)) / fd[:, None], "e2m1")
    return {
        "keys_words": keysp[0],
        "keys_scales": keysp[1],
        "notes": (n((D, U)) * 1.0 / np.sqrt(D) * fd[:, None]).astype(np.float32),
        "more_words": morep[0],
        "more_scales": morep[1],
        "users2": (n((D, Z)) * 1.0 / np.sqrt(D) * fd[:, None]).astype(np.float32),
        "rowf": (np.random.uniform(0.02, 0.08, (I, 1)) * fi[:, None]).astype(np.float32),
        "vals": (n((E, T)) / ti).astype(np.float32),
        "mem": (np.random.uniform(0.3, 1.0, (1, J))).astype(np.float32),
        "offs": striped(idx),
        "offs2": striped(idx2),
        "offs3": striped(idx3),
        "offs4": striped(idx4),
    }


def reference(keys_words, keys_scales, notes, more_words, more_scales, users2, rowf, vals, mem, offs, offs2, offs3, offs4):
    idx = unstriped(offs)
    idx2 = unstriped(offs2)
    idx3 = unstriped(offs3)
    idx4 = unstriped(offs4)
    keysu = unpack_weight(keys_words, keys_scales, "e2m1")
    moreu = unpack_weight(more_words, more_scales, "e2m1")
    keysidxg = keysu[:, idx]
    notesidx2q = mxq(f64(notes)[:, idx2], 0, "e4m3")
    moreidx3g = moreu[:, idx3]
    users2idx4q = mxq(f64(users2)[:, idx4], 0, "e4m3")
    g9 = keysidxg.T @ notesidx2q + moreidx3g.T @ users2idx4q
    g0 = np.maximum(g9, 0.0)
    gr1 = g0 * f64(rowf)
    vt1 = f64(vals)[:, idx].T
    vt1q = mxq(vt1, 0, "e4m3")
    gr1q = mxq(gr1, 0, "e4m3")
    o = vt1q.T @ gr1q
    o1 = np.pad(o, ((0, 0), (1, 0)))[:, :J]
    y = o - o1 * f64(mem)
    words, scales = planes(y)
    return y, words, scales

@@ -1,0 +1,223 @@
+from contextlib import ExitStack
+
+import concourse.mybir as mybir
+from concourse.masks import make_identity
+
+D, T, I, J, U, X, Z, E = 512, 2048, 512, 512, 1024, 1024, 1024, 512
+FLOPS = 2 * D * I * J * 2 + 2 * I * E * J
+
+F32 = mybir.dt.float32
+BF16 = mybir.dt.bfloat16
+I32 = mybir.dt.int32
+U32 = mybir.dt.uint32
+U16 = mybir.dt.uint16
+U8 = mybir.dt.uint8
+FP8X4 = mybir.dt.float8_e4m3fn_x4
+FP4X4 = mybir.dt.float4_e2m1fn_x4
+ALU = mybir.AluOpType
+COPY = mybir.ActivationFunctionType.Copy
+
+P = 128
+PACK = 4
+HALF = J // 2
+CHUNK = 128
+
+
+def tile_attend_tab_twosum_changes_pl_kernel(tc, keys_words, keys_scales, notes, more_words, more_scales, users2, rowf, vals, mem,
+                                              offs, offs2, offs3, offs4, out_0, out_1, out_2):
+    nc = tc.nc
+    with ExitStack() as ctx:
+        lists = ctx.enter_context(tc.tile_pool(name="lists", bufs=1))
+        sb = ctx.enter_context(tc.tile_pool(name="sb", bufs=1))
+        ps = ctx.enter_context(tc.psum_pool(name="ps", bufs=1))
+
+        def tile(shape, dtype, name):
+            return sb.tile(shape, dtype, name=name, align_bytes=64)
+
+        def bank(shape, number, name):
+            return ps.tile(shape, F32, name=name, tag="bank%d" % number)
+
+        def load_list(src, name):
+            dst = lists.tile([P, I // 16], U16, name=name)
+            nc.sync.dma_start(dst[:], src)
+            return dst
+
+        def load_plane(src, t, name):
+            dst = tile([P, src.shape[1]], F32, name)
+            nc.sync.dma_start(out=dst[:], in_=src.rearrange("(p t) c -> p t c", t=PACK)[:, t, :])
+            return dst
+
+        def load_words(src, width, name):
+            dst = tile([P, width], U16, name)
+            nc.sync.dma_start(out=dst[:].bitcast(I32), in_=src[0].bitcast(I32))
+            return dst
+
+        def zeroed(width, name):
+            dst = tile([P, width], U8, name)
+            nc.vector.memset(dst[:].bitcast(I32), 0)
+            return dst
+
+        def load_scale_rows(dst, src, quadrants):
+            for q in quadrants:
+                nc.sync.dma_start(out=dst[32 * q : 32 * q + 4, :].bitcast(I32), in_=src[0, 4 * q : 4 * q + 4, :].bitcast(I32))
+
+        key_scale_pool = zeroed(T, "key_scale_pool")
+        more_scale_pool = zeroed(X, "more_scale_pool")
+        row_factor = tile([P, PACK], F32, "row_factor")
+        nc.gpsimd.dma_start(out=row_factor[:], in_=rowf.rearrange("(p t) o -> p (t o)", t=PACK))
+        mem_cols = tile([P, PACK], F32, "mem_cols")
+        nc.gpsimd.dma_start(out=mem_cols[:], in_=mem.rearrange("o (p t) -> (o p) t", t=PACK))
+        ident = tile([P, P], F32, "ident")
+        make_identity(nc, ident[:])
+
+        note_list = load_list(offs2, "note_list")
+        note_pool = [load_plane(notes, 0, "note_pool0")]
+        token_list = load_list(offs, "token_list")
+        key_word_pool = load_words(keys_words, T, "key_word_pool")
+        note_pool.append(load_plane(notes, 1, "note_pool1"))
+        more_list = load_list(offs3, "more_list")
+        note_pool.append(load_plane(notes, 2, "note_pool2"))
+        more_word_pool = load_words(more_words, X, "more_word_pool")
+        load_scale_rows(key_scale_pool, keys_scales, (0, 1))
+        note_pool.append(load_plane(notes, 3, "note_pool3"))
+        load_scale_rows(key_scale_pool, keys_scales, (2, 3))
+        user_list = load_list(offs4, "user_list")
+        user_pool = [load_plane(users2, 0, "user_pool0")]
+        load_scale_rows(more_scale_pool, more_scales, (0, 1))
+        user_pool.append(load_plane(users2, 1, "user_pool1"))
+        load_scale_rows(more_scale_pool, more_scales, (2, 3))
+        user_pool.append(load_plane(users2, 2, "user_pool2"))
+        user_pool.append(load_plane(users2, 3, "user_pool3"))
+        val_pool = [load_plane(vals, t, "val_pool%d" % t) for t in range(PACK)]
+
+        def gather_words(pool, index, name):
+            picked = tile([P, I], U16, name + "_picked")
+            nc.vector.tensor_copy(picked[:], pool[:].indirect(index[:]))
+            dealt = tile([P, I], U16, name)
+            nc.vector.tensor_copy(out=dealt[:].rearrange("p (t s) -> p s t", t=PACK), in_=picked[:].rearrange("p (s t) -> p s t", t=PACK))
+            return dealt
+
+        def gather_scales(pool, index, name):
+            dealt = tile([P, I], U8, name)
+            nc.vector.tensor_copy(dealt[:].rearrange("p (t s) -> p s t", t=PACK), pool[:].indirect(index[:]))
+            return dealt
+
+        def interleave(engine_copy, dst, src):
+            engine_copy(out=dst.rearrange("p (c i t) -> p c t i", i=4, t=PACK), in_=src.rearrange("p t (c i) -> p c t i", i=4))
+
+        def quantize(codes, scales, src):
+            nc.vector.quantize_mx(out=codes.bitcast(FP8X4), scales=scales, in_=src)
+
+        note_picked = tile([P, PACK, J], BF16, "note_picked")
+        for t in range(PACK):
+            nc.scalar.activation(note_picked[:, t, :], note_pool[t][:].indirect(note_list[:]), COPY)
+
+        key_words = gather_words(key_word_pool, token_list, "key_words")
+        more_words_sb = gather_words(more_word_pool, more_list, "more_words_sb")
+        key_scales = gather_scales(key_scale_pool, token_list, "key_scales")
+
+        note_woven = tile([P, PACK * J], BF16, "note_woven")
+        interleave(nc.vector.tensor_copy, note_woven[:], note_picked[:])
+        note_codes = tile([P, J], U32, "note_codes")
+        note_scales = tile([P, J], U8, "note_scales")
+        quantize(note_codes[:], note_scales[:], note_woven[:])
+
+        more_scales_sb = gather_scales(more_scale_pool, more_list, "more_scales_sb")
+
+        table = [bank([P, PACK, CHUNK], c, "table%d" % c) for c in range(J // CHUNK)]
+
+        def table_passes(c, words, word_scales, codes, scales, c0, first):
+            for t in range(PACK):
+                rows = slice(t * P, (t + 1) * P)
+                cols = slice(c0, c0 + CHUNK)
+                nc.tensor.matmul_mx(out=table[c][:, t, :], lhsT=words[:, rows].bitcast(FP4X4), lhsT_scale=word_scales[:, rows],
+                                    rhs=codes[:, cols].bitcast(FP8X4), rhs_scale=scales[:, cols],
+                                    start=(first and t == 0), stop=(not first and t == PACK - 1))
+
+        for c in range(J // CHUNK):
+            table_passes(c, key_words, key_scales, note_codes, note_scales, c * CHUNK, True)
+
+        mem_bank = bank([P, PACK, P], 4, "mem_bank")
+        for t in range(PACK):
+            nc.tensor.transpose(mem_bank[:, t, :], mem_cols[:, t : t + 1].to_broadcast([P, P]), ident[:])
+
+        user_picked = [tile([P, PACK, HALF], BF16, "user_picked%d" % h) for h in range(2)]
+        for t in range(PACK):
+            for h in range(2):
+                window = user_pool[t][:].indirect(user_list[:, 16 * h : 16 * h + 16])
+                if t == PACK - 1 and h == 0:
+                    nc.vector.tensor_copy(user_picked[h][:, t, :], window)
+                else:
+                    nc.scalar.activation(user_picked[h][:, t, :], window, COPY)
+
+        mem_rows = tile([P, J], F32, "mem_rows")
+        nc.scalar.copy(out=mem_rows[:].rearrange("f (p t) -> f p t", t=PACK), in_=mem_bank[:].rearrange("f t p -> f p t"))
+
+        for h in range(2):
+            user_woven = tile([P, PACK * HALF], BF16, "user_woven%d" % h)
+            interleave(nc.vector.tensor_copy, user_woven[:], user_picked[h][:])
+            user_codes = tile([P, HALF], U32, "user_codes%d" % h)
+            user_scales = tile([P, HALF], U8, "user_scales%d" % h)
+            quantize(user_codes[:], user_scales[:], user_woven[:])
+            for c in range(2):
+                table_passes(2 * h + c, more_words_sb, more_scales_sb, user_codes, user_scales, c * CHUNK, False)
+
+        weight_codes = tile([P, J], U32, "weight_codes")
+        weight_scales = tile([P, J], U8, "weight_scales")
+        weight_woven = [tile([P, PACK * HALF], BF16, "weight_woven%d" % h) for h in range(2)]
+        for h in range(2):
+            for c in range(2):
+                nc.vector.scalar_tensor_tensor(
+                    out=weight_woven[h][:, c * CHUNK * PACK : (c + 1) * CHUNK * PACK].rearrange("p (j t) -> p j t", t=PACK),
+                    in0=table[2 * h + c][:].rearrange("p t j -> p j t"), scalar=0.0,
+                    in1=row_factor[:].unsqueeze(1).to_broadcast([P, CHUNK, PACK]), op0=ALU.max, op1=ALU.mult)
+        for h in range(2):
+            cols = slice(h * HALF, (h + 1) * HALF)
+            quantize(weight_codes[:, cols], weight_scales[:, cols], weight_woven[h][:])
+
+        result = [tile([P, PACK, HALF], F32, "result%d" % h) for h in range(2)]
+        out_rows = out_0.rearrange("(p t) j -> p t j", t=PACK)
+        o_banks = [(6, 7), (0, 1), (2, 3), (6, 7)]
+        for t in range(PACK):
+            val_picked = tile([P, I], BF16, "val_picked%d" % t)
+            nc.scalar.activation(val_picked[:], val_pool[t][:].indirect(token_list[:]), COPY)
+            pairs = val_picked[:].bitcast(F32)
+            turned = bank([P, 2, P], 4 + (t + 1) % 2, "turned%d" % t)
+            for u in range(2):
+                nc.tensor.transpose(turned[:, u, :], pairs[:, u : 2 * P : 2], ident[:])
+            val_woven = tile([P, PACK * P], BF16, "val_woven%d" % t)
+            nc.scalar.copy(out=val_woven[:].bitcast(F32).rearrange("p (e u) -> p e u", u=2), in_=turned[:].rearrange("p u e -> p e u"))
+            val_codes = tile([P, P], U32, "val_codes%d" % t)
+            val_scales = tile([P, P], U8, "val_scales%d" % t)
+            quantize(val_codes[:], val_scales[:], val_woven[:])
+            sums = [bank([P, HALF], o_banks[t][h], "sums%d_%d" % (t, h)) for h in range(2)]
+            for h in range(2):
+                cols = slice(h * HALF, (h + 1) * HALF)
+                nc.tensor.matmul_mx(out=sums[h][:], lhsT=val_codes[:].bitcast(FP8X4), lhsT_scale=val_scales[:],
+                                    rhs=weight_codes[:, cols].bitcast(FP8X4), rhs_scale=weight_scales[:, cols], start=True, stop=True)
+            carried = tile([P, J], F32, "carried%d" % t)
+            nc.vector.memset(carried[:, 0:1], 0.0)
+            nc.vector.tensor_tensor(carried[:, 1 : HALF + 1], sums[0][:], mem_rows[:, 1 : HALF + 1], ALU.mult)
+            nc.vector.tensor_tensor(carried[:, HALF + 1 : J], sums[1][:, 0 : HALF - 1], mem_rows[:, HALF + 1 : J], ALU.mult)
+            for h in range(2):
+                cols = slice(h * HALF, (h + 1) * HALF)
+                nc.vector.tensor_tensor(result[h][:, t, :], sums[h][:], carried[:, cols], ALU.subtract)
+            if t >= PACK - 2:
+                t0 = 0 if t == PACK - 2 else t
+                for h in range(2):
+                    cols = slice(h * HALF, (h + 1) * HALF)
+                    nc.sync.dma_start(out=out_rows[:, t0 : t + 1, cols], in_=result[h][:, t0 : t + 1, :])
+
+        out_codes = tile([P, J], U32, "out_codes")
+        out_scales = tile([P, J], U8, "out_scales")
+        out_words = out_1[0].rearrange("p c r -> p (c r)").bitcast(I32)
+        result_woven = [tile([P, PACK * HALF], BF16, "result_woven%d" % h) for h in range(2)]
+        interleave(nc.scalar.copy, result_woven[0][:], result[0][:])
+        interleave(nc.vector.tensor_copy, result_woven[1][:], result[1][:])
+        for h in range(2):
+            cols = slice(h * HALF, (h + 1) * HALF)
+            quantize(out_codes[:, cols], out_scales[:, cols], result_woven[h][:])
+            nc.sync.dma_start(out=out_words[:, cols], in_=out_codes[:, cols].bitcast(I32))
+        for q in range(4):
+            queue = nc.sync if q % 2 == 0 else nc.scalar
+            queue.dma_start(out=out_2[0, 4 * q : 4 * q + 4, :].bitcast(I32), in_=out_scales[32 * q : 32 * q + 4, :].bitcast(I32))

@@ -54,40 +54,37 @@ def tile_attend_tab_twosum_changes_pl_kernel(tc, keys_words, keys_scales, notes,
 
         def zeroed(width, name):
             dst = tile([P, width], U8, name)
-            nc.vector.memset(dst[:].bitcast(I32), 0)
+            nc.gpsimd.memset(dst[:].bitcast(I32), 0)
             return dst
 
-        def load_scale_rows(dst, src, quadrants):
+        def load_scale_rows(queue, dst, src, quadrants):
             for q in quadrants:
-                nc.sync.dma_start(out=dst[32 * q : 32 * q + 4, :].bitcast(I32), in_=src[0, 4 * q : 4 * q + 4, :].bitcast(I32))
+                queue.dma_start(out=dst[32 * q : 32 * q + 4, :].bitcast(I32), in_=src[0, 4 * q : 4 * q + 4, :].bitcast(I32))
 
-        key_scale_pool = zeroed(T, "key_scale_pool")
         more_scale_pool = zeroed(X, "more_scale_pool")
-        row_factor = tile([P, PACK], F32, "row_factor")
-        nc.gpsimd.dma_start(out=row_factor[:], in_=rowf.rearrange("(p t) o -> p (t o)", t=PACK))
+        key_scale_pool = zeroed(T, "key_scale_pool")
         mem_cols = tile([P, PACK], F32, "mem_cols")
         nc.gpsimd.dma_start(out=mem_cols[:], in_=mem.rearrange("o (p t) -> (o p) t", t=PACK))
+        row_factor = tile([P, PACK], F32, "row_factor")
+        nc.gpsimd.dma_start(out=row_factor[:], in_=rowf.rearrange("(p t) o -> p (t o)", t=PACK))
         ident = tile([P, P], F32, "ident")
         make_identity(nc, ident[:])
 
+        more_list = load_list(offs3, "more_list")
+        more_word_pool = load_words(more_words, X, "more_word_pool")
         note_list = load_list(offs2, "note_list")
         note_pool = [load_plane(notes, 0, "note_pool0")]
+        load_scale_rows(nc.sync, more_scale_pool, more_scales, (0, 1))
+        note_pool.append(load_plane(notes, 1, "note_pool1"))
+        load_scale_rows(nc.sync, more_scale_pool, more_scales, (2, 3))
         token_list = load_list(offs, "token_list")
         key_word_pool = load_words(keys_words, T, "key_word_pool")
-        note_pool.append(load_plane(notes, 1, "note_pool1"))
-        more_list = load_list(offs3, "more_list")
+        load_scale_rows(nc.sync, key_scale_pool, keys_scales, (0, 1))
         note_pool.append(load_plane(notes, 2, "note_pool2"))
-        more_word_pool = load_words(more_words, X, "more_word_pool")
-        load_scale_rows(key_scale_pool, keys_scales, (0, 1))
+        load_scale_rows(nc.sync, key_scale_pool, keys_scales, (2, 3))
         note_pool.append(load_plane(notes, 3, "note_pool3"))
-        load_scale_rows(key_scale_pool, keys_scales, (2, 3))
         user_list = load_list(offs4, "user_list")
-        user_pool = [load_plane(users2, 0, "user_pool0")]
-        load_scale_rows(more_scale_pool, more_scales, (0, 1))
-        user_pool.append(load_plane(users2, 1, "user_pool1"))
-        load_scale_rows(more_scale_pool, more_scales, (2, 3))
-        user_pool.append(load_plane(users2, 2, "user_pool2"))
-        user_pool.append(load_plane(users2, 3, "user_pool3"))
+        user_pool = [load_plane(users2, t, "user_pool%d" % t) for t in range(PACK)]
         val_pool = [load_plane(vals, t, "val_pool%d" % t) for t in range(PACK)]
 
         def gather_words(pool, index, name):
@@ -108,21 +105,24 @@ def tile_attend_tab_twosum_changes_pl_kernel(tc, keys_words, keys_scales, notes,
         def quantize(codes, scales, src):
             nc.vector.quantize_mx(out=codes.bitcast(FP8X4), scales=scales, in_=src)
 
-        note_picked = tile([P, PACK, J], BF16, "note_picked")
-        for t in range(PACK):
-            nc.scalar.activation(note_picked[:, t, :], note_pool[t][:].indirect(note_list[:]), COPY)
+        def weave_pair(engine_copy, dst, src, pair):
+            engine_copy(out=dst.rearrange("p (c i t) -> p c t i", i=4, t=PACK)[:, :, 2 * pair : 2 * pair + 2, :], in_=src.rearrange("p u (c i) -> p c u i", i=4))
 
-        key_words = gather_words(key_word_pool, token_list, "key_words")
         more_words_sb = gather_words(more_word_pool, more_list, "more_words_sb")
+        more_scales_sb = gather_scales(more_scale_pool, more_list, "more_scales_sb")
+        key_words = gather_words(key_word_pool, token_list, "key_words")
         key_scales = gather_scales(key_scale_pool, token_list, "key_scales")
+
+        note_picked = tile([P, PACK, J], BF16, "note_picked")
+        for t in range(PACK - 1):
+            nc.scalar.activation(note_picked[:, t, :], note_pool[t][:].indirect(note_list[:]), COPY)
+        nc.vector.tensor_copy(note_picked[:, PACK - 1, :], note_pool[PACK - 1][:].indirect(note_list[:]))
 
         note_woven = tile([P, PACK * J], BF16, "note_woven")
         interleave(nc.vector.tensor_copy, note_woven[:], note_picked[:])
         note_codes = tile([P, J], U32, "note_codes")
         note_scales = tile([P, J], U8, "note_scales")
         quantize(note_codes[:], note_scales[:], note_woven[:])
-
-        more_scales_sb = gather_scales(more_scale_pool, more_list, "more_scales_sb")
 
         table = [bank([P, PACK, CHUNK], c, "table%d" % c) for c in range(J // CHUNK)]
 
@@ -141,82 +141,123 @@ def tile_attend_tab_twosum_changes_pl_kernel(tc, keys_words, keys_scales, notes,
         for t in range(PACK):
             nc.tensor.transpose(mem_bank[:, t, :], mem_cols[:, t : t + 1].to_broadcast([P, P]), ident[:])
 
-        user_picked = [tile([P, PACK, HALF], BF16, "user_picked%d" % h) for h in range(2)]
-        for t in range(PACK):
-            for h in range(2):
-                window = user_pool[t][:].indirect(user_list[:, 16 * h : 16 * h + 16])
-                if t == PACK - 1 and h == 0:
-                    nc.vector.tensor_copy(user_picked[h][:, t, :], window)
-                else:
-                    nc.scalar.activation(user_picked[h][:, t, :], window, COPY)
+        user_low = tile([P, 2, J], BF16, "user_low")
+        for t in range(2):
+            nc.scalar.activation(user_low[:, t, :], user_pool[t][:].indirect(user_list[:]), COPY)
+        user_woven = tile([P, PACK * J], BF16, "user_woven")
+        user_high = [tile([P, 2, HALF], BF16, "user_high%d" % h) for h in range(2)]
+        weave_pair(nc.vector.tensor_copy, user_woven[:], user_low[:], 0)
+        for h in range(2):
+            nc.scalar.activation(user_high[h][:, 0, :], user_pool[2][:].indirect(user_list[:, 16 * h : 16 * h + 16]), COPY)
+        nc.vector.tensor_copy(user_high[0][:, 1, :], user_pool[3][:].indirect(user_list[:, 0:16]))
+        nc.scalar.activation(user_high[1][:, 1, :], user_pool[3][:].indirect(user_list[:, 16:32]), COPY)
 
         mem_rows = tile([P, J], F32, "mem_rows")
         nc.scalar.copy(out=mem_rows[:].rearrange("f (p t) -> f p t", t=PACK), in_=mem_bank[:].rearrange("f t p -> f p t"))
 
         for h in range(2):
-            user_woven = tile([P, PACK * HALF], BF16, "user_woven%d" % h)
-            interleave(nc.vector.tensor_copy, user_woven[:], user_picked[h][:])
+            woven_half = user_woven[:, h * PACK * HALF : (h + 1) * PACK * HALF]
+            weave_pair(nc.vector.tensor_copy, woven_half, user_high[h][:], 1)
             user_codes = tile([P, HALF], U32, "user_codes%d" % h)
             user_scales = tile([P, HALF], U8, "user_scales%d" % h)
-            quantize(user_codes[:], user_scales[:], user_woven[:])
+            quantize(user_codes[:], user_scales[:], woven_half)
             for c in range(2):
                 table_passes(2 * h + c, more_words_sb, more_scales_sb, user_codes, user_scales, c * CHUNK, False)
 
-        weight_codes = tile([P, J], U32, "weight_codes")
-        weight_scales = tile([P, J], U8, "weight_scales")
+        weight_codes = [tile([P, HALF], U32, "weight_codes%d" % h) for h in range(2)]
+        weight_scales = [tile([P, HALF], U8, "weight_scales%d" % h) for h in range(2)]
         weight_woven = [tile([P, PACK * HALF], BF16, "weight_woven%d" % h) for h in range(2)]
-        for h in range(2):
-            for c in range(2):
-                nc.vector.scalar_tensor_tensor(
-                    out=weight_woven[h][:, c * CHUNK * PACK : (c + 1) * CHUNK * PACK].rearrange("p (j t) -> p j t", t=PACK),
-                    in0=table[2 * h + c][:].rearrange("p t j -> p j t"), scalar=0.0,
-                    in1=row_factor[:].unsqueeze(1).to_broadcast([P, CHUNK, PACK]), op0=ALU.max, op1=ALU.mult)
-        for h in range(2):
-            cols = slice(h * HALF, (h + 1) * HALF)
-            quantize(weight_codes[:, cols], weight_scales[:, cols], weight_woven[h][:])
 
-        result = [tile([P, PACK, HALF], F32, "result%d" % h) for h in range(2)]
+        def weigh(c):
+            nc.vector.scalar_tensor_tensor(
+                out=weight_woven[c // 2][:, c % 2 * CHUNK * PACK : (c % 2 + 1) * CHUNK * PACK].rearrange("p (j t) -> p j t", t=PACK),
+                in0=table[c][:].rearrange("p t j -> p j t"), scalar=0.0,
+                in1=row_factor[:].unsqueeze(1).to_broadcast([P, CHUNK, PACK]), op0=ALU.max, op1=ALU.mult)
+
+        result_low = tile([P, 2, J], F32, "result_low")
+        result_high = [tile([P, 2, HALF], F32, "result_high%d" % h) for h in range(2)]
         out_rows = out_0.rearrange("(p t) j -> p t j", t=PACK)
-        o_banks = [(6, 7), (0, 1), (2, 3), (6, 7)]
-        for t in range(PACK):
-            val_picked = tile([P, I], BF16, "val_picked%d" % t)
+        halves = [slice(0, HALF), slice(HALF, J)]
+
+        def turn_values(t, woven):
+            val_picked = sb.tile([P, I], BF16, name="val_picked%d" % t, tag="val_picked%d" % t, align_bytes=64)
             nc.scalar.activation(val_picked[:], val_pool[t][:].indirect(token_list[:]), COPY)
             pairs = val_picked[:].bitcast(F32)
-            turned = bank([P, 2, P], 4 + (t + 1) % 2, "turned%d" % t)
+            turned = bank([P, 2, P], (5, 4, 5, 5)[t], "turned%d" % t)
             for u in range(2):
                 nc.tensor.transpose(turned[:, u, :], pairs[:, u : 2 * P : 2], ident[:])
-            val_woven = tile([P, PACK * P], BF16, "val_woven%d" % t)
-            nc.scalar.copy(out=val_woven[:].bitcast(F32).rearrange("p (e u) -> p e u", u=2), in_=turned[:].rearrange("p u e -> p e u"))
-            val_codes = tile([P, P], U32, "val_codes%d" % t)
-            val_scales = tile([P, P], U8, "val_scales%d" % t)
-            quantize(val_codes[:], val_scales[:], val_woven[:])
-            sums = [bank([P, HALF], o_banks[t][h], "sums%d_%d" % (t, h)) for h in range(2)]
-            for h in range(2):
-                cols = slice(h * HALF, (h + 1) * HALF)
-                nc.tensor.matmul_mx(out=sums[h][:], lhsT=val_codes[:].bitcast(FP8X4), lhsT_scale=val_scales[:],
-                                    rhs=weight_codes[:, cols].bitcast(FP8X4), rhs_scale=weight_scales[:, cols], start=True, stop=True)
-            carried = tile([P, J], F32, "carried%d" % t)
-            nc.vector.memset(carried[:, 0:1], 0.0)
-            nc.vector.tensor_tensor(carried[:, 1 : HALF + 1], sums[0][:], mem_rows[:, 1 : HALF + 1], ALU.mult)
-            nc.vector.tensor_tensor(carried[:, HALF + 1 : J], sums[1][:, 0 : HALF - 1], mem_rows[:, HALF + 1 : J], ALU.mult)
-            for h in range(2):
-                cols = slice(h * HALF, (h + 1) * HALF)
-                nc.vector.tensor_tensor(result[h][:, t, :], sums[h][:], carried[:, cols], ALU.subtract)
-            if t >= PACK - 2:
-                t0 = 0 if t == PACK - 2 else t
-                for h in range(2):
-                    cols = slice(h * HALF, (h + 1) * HALF)
-                    nc.sync.dma_start(out=out_rows[:, t0 : t + 1, cols], in_=result[h][:, t0 : t + 1, :])
+            nc.scalar.copy(out=woven.bitcast(F32).rearrange("p (e u) -> p e u", u=2), in_=turned[:].rearrange("p u e -> p e u"))
 
+        def quantize_values(t, woven):
+            codes = tile([P, P], U32, "val_codes%d" % t)
+            scales = tile([P, P], U8, "val_scales%d" % t)
+            quantize(codes[:], scales[:], woven)
+            return codes, scales
+
+        def multiply(t, quantized, h):
+            sums = bank([P, HALF], ((6, 4), (0, 1), (2, 3), (7, 6))[t][h], "sums%d_%d" % (t, h))
+            nc.tensor.matmul_mx(out=sums[:], lhsT=quantized[0][:].bitcast(FP8X4), lhsT_scale=quantized[1][:],
+                                rhs=weight_codes[h][:].bitcast(FP8X4), rhs_scale=weight_scales[h][:], start=True, stop=True)
+            return sums
+
+        carried = [tile([P, J + 16], F32, "carried%d" % t) for t in range(PACK)]
+        for t in range(PACK):
+            nc.vector.memset(carried[t][:, 0:1], 0.0)
+
+        def carry(t, sums, h):
+            first, last = h * HALF + 1, min((h + 1) * HALF + 1, J)
+            nc.vector.tensor_tensor(carried[t][:, first:last], sums[:, 0 : last - first], mem_rows[:, first:last], ALU.mult)
+
+        def result_rows(t, h):
+            return result_low[:, t, halves[h]] if t < 2 else result_high[h][:, t - 2, :]
+
+        def subtract(t, sums, h):
+            nc.vector.tensor_tensor(result_rows(t, h), sums[:], carried[t][:, halves[h]], ALU.subtract)
+
+        val_woven = [
+            tile([P, PACK * P], BF16, "val_woven0")[:],
+            carried[0][:, HALF:J].bitcast(BF16),
+            carried[1][:, HALF + 16 : J + 16].bitcast(BF16),
+            result_rows(2, 0).bitcast(BF16),
+        ]
+
+        def prepare_values(t):
+            turn_values(t, val_woven[t])
+            return quantize_values(t, val_woven[t])
+
+        for c in range(3):
+            weigh(c)
+        quantize(weight_codes[0][:], weight_scales[0][:], weight_woven[0][:])
+        quantized = [prepare_values(0)]
+        weigh(3)
+        quantize(weight_codes[1][:], weight_scales[1][:], weight_woven[1][:])
+        for t in range(PACK):
+            sums = [multiply(t, quantized[t], 0)]
+            if t == 0:
+                quantized.append(prepare_values(1))
+            sums.append(multiply(t, quantized[t], 1))
+            carry(t, sums[0], 0)
+            if t == 1:
+                quantized.append(prepare_values(2))
+            carry(t, sums[1], 1)
+            if t == 2:
+                quantized.append(prepare_values(3))
+            for h in range(2):
+                subtract(t, sums[h], h)
+            if t == 1:
+                nc.sync.dma_start(out=out_rows[:, 0:2, :], in_=result_low[:])
+        for h in range(2):
+            nc.sync.dma_start(out=out_rows[:, 2:4, halves[h]], in_=result_high[h][:])
         out_codes = tile([P, J], U32, "out_codes")
         out_scales = tile([P, J], U8, "out_scales")
         out_words = out_1[0].rearrange("p c r -> p (c r)").bitcast(I32)
-        result_woven = [tile([P, PACK * HALF], BF16, "result_woven%d" % h) for h in range(2)]
-        interleave(nc.scalar.copy, result_woven[0][:], result[0][:])
-        interleave(nc.vector.tensor_copy, result_woven[1][:], result[1][:])
+        result_woven = sb.tile([P, PACK * J], BF16, name="result_woven", tag="val_picked%d" % (PACK - 1), align_bytes=64)
+        weave_pair(nc.scalar.copy, result_woven[:], result_low[:], 0)
+        for h in range(2):
+            weave_pair(nc.vector.tensor_copy, result_woven[:, h * PACK * HALF : (h + 1) * PACK * HALF], result_high[h][:], 1)
         for h in range(2):
             cols = slice(h * HALF, (h + 1) * HALF)
-            quantize(out_codes[:, cols], out_scales[:, cols], result_woven[h][:])
+            quantize(out_codes[:, cols], out_scales[:, cols], result_woven[:, h * PACK * HALF : (h + 1) * PACK * HALF])
             nc.sync.dma_start(out=out_words[:, cols], in_=out_codes[:, cols].bitcast(I32))
         for q in range(4):
             queue = nc.sync if q % 2 == 0 else nc.scalar

@@ -43,7 +43,7 @@ def tile_attend_tab_twosum_changes_pl_kernel(tc, keys_words, keys_scales, notes,
             return dst
 
         def load_plane(src, t, name):
-            dst = tile([P, src.shape[1]], F32, name)
+            dst = sb.tile([P, src.shape[1]], F32, name=name, tag=name, align_bytes=64)
             nc.sync.dma_start(out=dst[:], in_=src.rearrange("(p t) c -> p t c", t=PACK)[:, t, :])
             return dst
 
@@ -67,7 +67,7 @@ def tile_attend_tab_twosum_changes_pl_kernel(tc, keys_words, keys_scales, notes,
         nc.gpsimd.dma_start(out=mem_cols[:], in_=mem.rearrange("o (p t) -> (o p) t", t=PACK))
         row_factor = tile([P, PACK], F32, "row_factor")
         nc.gpsimd.dma_start(out=row_factor[:], in_=rowf.rearrange("(p t) o -> p (t o)", t=PACK))
-        ident = tile([P, P], F32, "ident")
+        ident = sb.tile([P, P], F32, name="ident", tag="ident", align_bytes=64)
         make_identity(nc, ident[:])
 
         more_list = load_list(offs3, "more_list")
@@ -116,7 +116,8 @@ def tile_attend_tab_twosum_changes_pl_kernel(tc, keys_words, keys_scales, notes,
         note_picked = tile([P, PACK, J], BF16, "note_picked")
         for t in range(PACK - 1):
             nc.scalar.activation(note_picked[:, t, :], note_pool[t][:].indirect(note_list[:]), COPY)
-        nc.vector.tensor_copy(note_picked[:, PACK - 1, :], note_pool[PACK - 1][:].indirect(note_list[:]))
+        nc.scalar.activation(note_picked[:, PACK - 1, 0:HALF], note_pool[PACK - 1][:].indirect(note_list[:, 0:16]), COPY)
+        nc.vector.tensor_copy(note_picked[:, PACK - 1, HALF:J], note_pool[PACK - 1][:].indirect(note_list[:, 16:32]))
 
         note_woven = tile([P, PACK * J], BF16, "note_woven")
         interleave(nc.vector.tensor_copy, note_woven[:], note_picked[:])
@@ -141,26 +142,25 @@ def tile_attend_tab_twosum_changes_pl_kernel(tc, keys_words, keys_scales, notes,
         for t in range(PACK):
             nc.tensor.transpose(mem_bank[:, t, :], mem_cols[:, t : t + 1].to_broadcast([P, P]), ident[:])
 
-        user_low = tile([P, 2, J], BF16, "user_low")
-        for t in range(2):
-            nc.scalar.activation(user_low[:, t, :], user_pool[t][:].indirect(user_list[:]), COPY)
-        user_woven = tile([P, PACK * J], BF16, "user_woven")
-        user_high = [tile([P, 2, HALF], BF16, "user_high%d" % h) for h in range(2)]
-        weave_pair(nc.vector.tensor_copy, user_woven[:], user_low[:], 0)
-        for h in range(2):
-            nc.scalar.activation(user_high[h][:, 0, :], user_pool[2][:].indirect(user_list[:, 16 * h : 16 * h + 16]), COPY)
-        nc.vector.tensor_copy(user_high[0][:, 1, :], user_pool[3][:].indirect(user_list[:, 0:16]))
-        nc.scalar.activation(user_high[1][:, 1, :], user_pool[3][:].indirect(user_list[:, 16:32]), COPY)
+        user_picked = [tile([P, PACK, HALF], BF16, "user_picked%d" % h) for h in range(2)]
+        for t in range(PACK):
+            for h in range(2):
+                window = user_pool[t][:].indirect(user_list[:, 16 * h : 16 * h + 16])
+                if t == PACK - 1 and h == 1:
+                    nc.vector.tensor_copy(user_picked[h][:, t, :], window)
+                else:
+                    nc.scalar.activation(user_picked[h][:, t, :], window, COPY)
 
         mem_rows = tile([P, J], F32, "mem_rows")
         nc.scalar.copy(out=mem_rows[:].rearrange("f (p t) -> f p t", t=PACK), in_=mem_bank[:].rearrange("f t p -> f p t"))
 
+        user_woven = [tile([P, PACK * HALF], BF16, "user_woven%d" % h) for h in range(2)]
         for h in range(2):
-            woven_half = user_woven[:, h * PACK * HALF : (h + 1) * PACK * HALF]
-            weave_pair(nc.vector.tensor_copy, woven_half, user_high[h][:], 1)
+            interleave(nc.vector.tensor_copy, user_woven[h][:], user_picked[h][:])
+        for h in range(2):
             user_codes = tile([P, HALF], U32, "user_codes%d" % h)
             user_scales = tile([P, HALF], U8, "user_scales%d" % h)
-            quantize(user_codes[:], user_scales[:], woven_half)
+            quantize(user_codes[:], user_scales[:], user_woven[h][:])
             for c in range(2):
                 table_passes(2 * h + c, more_words_sb, more_scales_sb, user_codes, user_scales, c * CHUNK, False)
 
@@ -179,13 +179,16 @@ def tile_attend_tab_twosum_changes_pl_kernel(tc, keys_words, keys_scales, notes,
         out_rows = out_0.rearrange("(p t) j -> p t j", t=PACK)
         halves = [slice(0, HALF), slice(HALF, J)]
 
-        def turn_values(t, woven):
+        def turn_values(t):
             val_picked = sb.tile([P, I], BF16, name="val_picked%d" % t, tag="val_picked%d" % t, align_bytes=64)
             nc.scalar.activation(val_picked[:], val_pool[t][:].indirect(token_list[:]), COPY)
             pairs = val_picked[:].bitcast(F32)
-            turned = bank([P, 2, P], (5, 4, 5, 5)[t], "turned%d" % t)
+            turned = bank([P, 2, P], (5, 4, 5, 4)[t], "turned%d" % t)
             for u in range(2):
                 nc.tensor.transpose(turned[:, u, :], pairs[:, u : 2 * P : 2], ident[:])
+            return turned
+
+        def copy_turned(turned, woven):
             nc.scalar.copy(out=woven.bitcast(F32).rearrange("p (e u) -> p e u", u=2), in_=turned[:].rearrange("p u e -> p e u"))
 
         def quantize_values(t, woven):
@@ -195,12 +198,12 @@ def tile_attend_tab_twosum_changes_pl_kernel(tc, keys_words, keys_scales, notes,
             return codes, scales
 
         def multiply(t, quantized, h):
-            sums = bank([P, HALF], ((6, 4), (0, 1), (2, 3), (7, 6))[t][h], "sums%d_%d" % (t, h))
+            sums = bank([P, HALF], ((6, 7), (0, 1), (2, 3), (6, 7))[t][h], "sums%d_%d" % (t, h))
             nc.tensor.matmul_mx(out=sums[:], lhsT=quantized[0][:].bitcast(FP8X4), lhsT_scale=quantized[1][:],
                                 rhs=weight_codes[h][:].bitcast(FP8X4), rhs_scale=weight_scales[h][:], start=True, stop=True)
             return sums
 
-        carried = [tile([P, J + 16], F32, "carried%d" % t) for t in range(PACK)]
+        carried = [tile([P, J], F32, "carried%d" % t) for t in range(PACK)]
         for t in range(PACK):
             nc.vector.memset(carried[t][:, 0:1], 0.0)
 
@@ -214,34 +217,31 @@ def tile_attend_tab_twosum_changes_pl_kernel(tc, keys_words, keys_scales, notes,
         def subtract(t, sums, h):
             nc.vector.tensor_tensor(result_rows(t, h), sums[:], carried[t][:, halves[h]], ALU.subtract)
 
-        val_woven = [
-            tile([P, PACK * P], BF16, "val_woven0")[:],
-            carried[0][:, HALF:J].bitcast(BF16),
-            carried[1][:, HALF + 16 : J + 16].bitcast(BF16),
-            result_rows(2, 0).bitcast(BF16),
-        ]
+        def woven_in_pool_slot(t):
+            return sb.tile([P, PACK * P], BF16, name="val_woven%d" % t, tag="val_pool%d" % (t + 1), align_bytes=64)[:]
 
-        def prepare_values(t):
-            turn_values(t, val_woven[t])
-            return quantize_values(t, val_woven[t])
+        def finish_values(t, turned, woven):
+            copy_turned(turned, woven)
+            return quantize_values(t, woven)
 
+        turned = [turn_values(0), turn_values(1)]
         for c in range(3):
             weigh(c)
         quantize(weight_codes[0][:], weight_scales[0][:], weight_woven[0][:])
-        quantized = [prepare_values(0)]
+        quantized = [finish_values(0, turned[0], woven_in_pool_slot(0))]
         weigh(3)
         quantize(weight_codes[1][:], weight_scales[1][:], weight_woven[1][:])
         for t in range(PACK):
-            sums = [multiply(t, quantized[t], 0)]
-            if t == 0:
-                quantized.append(prepare_values(1))
-            sums.append(multiply(t, quantized[t], 1))
-            carry(t, sums[0], 0)
+            sums = [multiply(t, quantized[t], h) for h in range(2)]
             if t == 1:
-                quantized.append(prepare_values(2))
-            carry(t, sums[1], 1)
+                quantized.append(finish_values(2, turned[2], carried[1][:, HALF:J].bitcast(BF16)))
+            for h in range(2):
+                carry(t, sums[h], h)
+            if t == 0:
+                turned.append(turn_values(2))
+                quantized.append(finish_values(1, turned[1], woven_in_pool_slot(1)))
             if t == 2:
-                quantized.append(prepare_values(3))
+                quantized.append(finish_values(3, turn_values(3), result_rows(2, 0).bitcast(BF16)))
             for h in range(2):
                 subtract(t, sums[h], h)
             if t == 1:
@@ -251,14 +251,15 @@ def tile_attend_tab_twosum_changes_pl_kernel(tc, keys_words, keys_scales, notes,
         out_codes = tile([P, J], U32, "out_codes")
         out_scales = tile([P, J], U8, "out_scales")
         out_words = out_1[0].rearrange("p c r -> p (c r)").bitcast(I32)
-        result_woven = sb.tile([P, PACK * J], BF16, name="result_woven", tag="val_picked%d" % (PACK - 1), align_bytes=64)
-        weave_pair(nc.scalar.copy, result_woven[:], result_low[:], 0)
+        result_woven = [sb.tile([P, PACK * HALF], BF16, name="result_woven%d" % h, tag=tag, align_bytes=64)
+                        for h, tag in enumerate(("val_picked3", "ident"))]
+        for h in (1, 0):
+            weave_pair(nc.scalar.copy, result_woven[h][:], result_low[:, :, halves[h]], 0)
+        weave_pair(nc.scalar.copy, result_woven[0][:], result_high[0][:], 1)
+        weave_pair(nc.vector.tensor_copy, result_woven[1][:], result_high[1][:], 1)
         for h in range(2):
-            weave_pair(nc.vector.tensor_copy, result_woven[:, h * PACK * HALF : (h + 1) * PACK * HALF], result_high[h][:], 1)
-        for h in range(2):
-            cols = slice(h * HALF, (h + 1) * HALF)
-            quantize(out_codes[:, cols], out_scales[:, cols], result_woven[:, h * PACK * HALF : (h + 1) * PACK * HALF])
-            nc.sync.dma_start(out=out_words[:, cols], in_=out_codes[:, cols].bitcast(I32))
+            quantize(out_codes[:, halves[h]], out_scales[:, halves[h]], result_woven[h][:])
+            nc.sync.dma_start(out=out_words[:, halves[h]], in_=out_codes[:, halves[h]].bitcast(I32))
         for q in range(4):
             queue = nc.sync if q % 2 == 0 else nc.scalar
             queue.dma_start(out=out_2[0, 4 * q : 4 * q + 4, :].bitcast(I32), in_=out_scales[32 * q : 32 * q + 4, :].bitcast(I32))

@@ -70,6 +70,12 @@ def tile_attend_tab_twosum_changes_pl_kernel(tc, keys_words, keys_scales, notes,
         ident = sb.tile([P, P], F32, name="ident", tag="ident", align_bytes=64)
         make_identity(nc, ident[:])
 
+        zero = tile([P, 1], F32, "zero")
+        nc.vector.memset(zero[:], 0.0)
+        carried = [tile([P, J + 16], F32, "carried%d" % t) for t in range(PACK)]
+        for t in range(PACK):
+            nc.scalar.activation(carried[t][:, 0:1], zero[:], COPY)
+
         more_list = load_list(offs3, "more_list")
         more_word_pool = load_words(more_words, X, "more_word_pool")
         note_list = load_list(offs2, "note_list")
@@ -146,7 +152,7 @@ def tile_attend_tab_twosum_changes_pl_kernel(tc, keys_words, keys_scales, notes,
         for t in range(PACK):
             for h in range(2):
                 window = user_pool[t][:].indirect(user_list[:, 16 * h : 16 * h + 16])
-                if t == PACK - 1 and h == 1:
+                if t >= 2 and h == 1:
                     nc.vector.tensor_copy(user_picked[h][:, t, :], window)
                 else:
                     nc.scalar.activation(user_picked[h][:, t, :], window, COPY)
@@ -155,9 +161,9 @@ def tile_attend_tab_twosum_changes_pl_kernel(tc, keys_words, keys_scales, notes,
         nc.scalar.copy(out=mem_rows[:].rearrange("f (p t) -> f p t", t=PACK), in_=mem_bank[:].rearrange("f t p -> f p t"))
 
         user_woven = [tile([P, PACK * HALF], BF16, "user_woven%d" % h) for h in range(2)]
-        for h in range(2):
-            interleave(nc.vector.tensor_copy, user_woven[h][:], user_picked[h][:])
-        for h in range(2):
+        interleave(nc.scalar.copy, user_woven[0][:], user_picked[0][:])
+        interleave(nc.vector.tensor_copy, user_woven[1][:], user_picked[1][:])
+        for h in (1, 0):
             user_codes = tile([P, HALF], U32, "user_codes%d" % h)
             user_scales = tile([P, HALF], U8, "user_scales%d" % h)
             quantize(user_codes[:], user_scales[:], user_woven[h][:])
@@ -203,9 +209,6 @@ def tile_attend_tab_twosum_changes_pl_kernel(tc, keys_words, keys_scales, notes,
                                 rhs=weight_codes[h][:].bitcast(FP8X4), rhs_scale=weight_scales[h][:], start=True, stop=True)
             return sums
 
-        carried = [tile([P, J], F32, "carried%d" % t) for t in range(PACK)]
-        for t in range(PACK):
-            nc.vector.memset(carried[t][:, 0:1], 0.0)
 
         def carry(t, sums, h):
             first, last = h * HALF + 1, min((h + 1) * HALF + 1, J)
@@ -224,19 +227,21 @@ def tile_attend_tab_twosum_changes_pl_kernel(tc, keys_words, keys_scales, notes,
             copy_turned(turned, woven)
             return quantize_values(t, woven)
 
-        turned = [turn_values(0), turn_values(1)]
-        for c in range(3):
+        for c in (2, 3, 0):
             weigh(c)
-        quantize(weight_codes[0][:], weight_scales[0][:], weight_woven[0][:])
-        quantized = [finish_values(0, turned[0], woven_in_pool_slot(0))]
-        weigh(3)
         quantize(weight_codes[1][:], weight_scales[1][:], weight_woven[1][:])
+        turned = [turn_values(0)]
+        quantized = [finish_values(0, turned[0], tile([P, PACK * P], BF16, "val_woven0")[:])]
+        turned.append(turn_values(1))
+        weigh(1)
+        quantize(weight_codes[0][:], weight_scales[0][:], weight_woven[0][:])
         for t in range(PACK):
-            sums = [multiply(t, quantized[t], h) for h in range(2)]
+            order = (1, 0) if t == 0 else (0, 1)
+            sums = {h: multiply(t, quantized[t], h) for h in order}
+            carry(t, sums[order[0]], order[0])
             if t == 1:
-                quantized.append(finish_values(2, turned[2], carried[1][:, HALF:J].bitcast(BF16)))
-            for h in range(2):
-                carry(t, sums[h], h)
+                quantized.append(finish_values(2, turned[2], carried[1][:, HALF + 16 : J + 16].bitcast(BF16)))
+            carry(t, sums[order[1]], order[1])
             if t == 0:
                 turned.append(turn_values(2))
                 quantized.append(finish_values(1, turned[1], woven_in_pool_slot(1)))
@@ -253,10 +258,10 @@ def tile_attend_tab_twosum_changes_pl_kernel(tc, keys_words, keys_scales, notes,
         out_words = out_1[0].rearrange("p c r -> p (c r)").bitcast(I32)
         result_woven = [sb.tile([P, PACK * HALF], BF16, name="result_woven%d" % h, tag=tag, align_bytes=64)
                         for h, tag in enumerate(("val_picked3", "ident"))]
-        for h in (1, 0):
+        for h in range(2):
             weave_pair(nc.scalar.copy, result_woven[h][:], result_low[:, :, halves[h]], 0)
-        weave_pair(nc.scalar.copy, result_woven[0][:], result_high[0][:], 1)
-        weave_pair(nc.vector.tensor_copy, result_woven[1][:], result_high[1][:], 1)
+        for h in range(2):
+            weave_pair(nc.vector.tensor_copy, result_woven[h][:], result_high[h][:], 1)
         for h in range(2):
             quantize(out_codes[:, halves[h]], out_scales[:, halves[h]], result_woven[h][:])
             nc.sync.dma_start(out=out_words[:, halves[h]], in_=out_codes[:, halves[h]].bitcast(I32))

@@ -58,8 +58,8 @@ def tile_attend_tab_twosum_changes_pl_kernel(tc, keys_words, keys_scales, notes,
             return dst
 
         def load_scale_rows(queue, dst, src, quadrants):
-            for q in quadrants:
-                queue.dma_start(out=dst[32 * q : 32 * q + 4, :].bitcast(I32), in_=src[0, 4 * q : 4 * q + 4, :].bitcast(I32))
+            for r in quadrants:
+                queue.dma_start(out=dst[r:P:32, :].bitcast(I32), in_=src[0, r:16:4, :].bitcast(I32))
 
         more_scale_pool = zeroed(X, "more_scale_pool")
         key_scale_pool = zeroed(T, "key_scale_pool")
@@ -267,4 +267,4 @@ def tile_attend_tab_twosum_changes_pl_kernel(tc, keys_words, keys_scales, notes,
             nc.sync.dma_start(out=out_words[:, halves[h]], in_=out_codes[:, halves[h]].bitcast(I32))
         for q in range(4):
             queue = nc.sync if q % 2 == 0 else nc.scalar
-            queue.dma_start(out=out_2[0, 4 * q : 4 * q + 4, :].bitcast(I32), in_=out_scales[32 * q : 32 * q + 4, :].bitcast(I32))
+            queue.dma_start(out=out_2[0, q:16:4, :].bitcast(I32), in_=out_scales[q:P:32, :].bitcast(I32))

from contextlib import ExitStack

import concourse.mybir as mybir
from concourse.masks import make_identity

D, T, I, J, U, X, Z, E = 512, 2048, 512, 512, 1024, 1024, 1024, 512
FLOPS = 2 * D * I * J * 2 + 2 * I * E * J

F32 = mybir.dt.float32
BF16 = mybir.dt.bfloat16
I32 = mybir.dt.int32
U32 = mybir.dt.uint32
U16 = mybir.dt.uint16
U8 = mybir.dt.uint8
FP8X4 = mybir.dt.float8_e4m3fn_x4
FP4X4 = mybir.dt.float4_e2m1fn_x4
ALU = mybir.AluOpType
COPY = mybir.ActivationFunctionType.Copy

P = 128
PACK = 4
HALF = J // 2
CHUNK = 128


def tile_attend_tab_twosum_changes_pl_kernel(tc, keys_words, keys_scales, notes, more_words, more_scales, users2, rowf, vals, mem,
                                              offs, offs2, offs3, offs4, out_0, out_1, out_2):
    nc = tc.nc
    with ExitStack() as ctx:
        lists = ctx.enter_context(tc.tile_pool(name="lists", bufs=1))
        sb = ctx.enter_context(tc.tile_pool(name="sb", bufs=1))
        ps = ctx.enter_context(tc.psum_pool(name="ps", bufs=1))

        def tile(shape, dtype, name):
            return sb.tile(shape, dtype, name=name, align_bytes=64)

        def bank(shape, number, name):
            return ps.tile(shape, F32, name=name, tag="bank%d" % number)

        def load_list(src, name):
            dst = lists.tile([P, I // 16], U16, name=name)
            nc.sync.dma_start(dst[:], src)
            return dst

        def load_plane(src, t, name):
            dst = sb.tile([P, src.shape[1]], F32, name=name, tag=name, align_bytes=64)
            nc.sync.dma_start(out=dst[:], in_=src.rearrange("(p t) c -> p t c", t=PACK)[:, t, :])
            return dst

        def load_words(src, width, name):
            dst = tile([P, width], U16, name)
            nc.sync.dma_start(out=dst[:].bitcast(I32), in_=src[0].bitcast(I32))
            return dst

        def zeroed(width, name):
            dst = tile([P, width], U8, name)
            nc.gpsimd.memset(dst[:].bitcast(I32), 0)
            return dst

        def load_scale_rows(queue, dst, src, quadrants):
            for r in quadrants:
                queue.dma_start(out=dst[r:P:32, :].bitcast(I32), in_=src[0, r:16:4, :].bitcast(I32))

        more_scale_pool = zeroed(X, "more_scale_pool")
        key_scale_pool = zeroed(T, "key_scale_pool")
        mem_cols = tile([P, PACK], F32, "mem_cols")
        nc.gpsimd.dma_start(out=mem_cols[:], in_=mem.rearrange("o (p t) -> (o p) t", t=PACK))
        row_factor = tile([P, PACK], F32, "row_factor")
        nc.gpsimd.dma_start(out=row_factor[:], in_=rowf.rearrange("(p t) o -> p (t o)", t=PACK))
        ident = sb.tile([P, P], F32, name="ident", tag="ident", align_bytes=64)
        make_identity(nc, ident[:])

        zero = tile([P, 1], F32, "zero")
        nc.vector.memset(zero[:], 0.0)
        carried = [tile([P, J + 16], F32, "carried%d" % t) for t in range(PACK)]
        for t in range(PACK):
            nc.scalar.activation(carried[t][:, 0:1], zero[:], COPY)

        more_list = load_list(offs3, "more_list")
        more_word_pool = load_words(more_words, X, "more_word_pool")
        note_list = load_list(offs2, "note_list")
        note_pool = [load_plane(notes, 0, "note_pool0")]
        load_scale_rows(nc.sync, more_scale_pool, more_scales, (0, 1))
        note_pool.append(load_plane(notes, 1, "note_pool1"))
        load_scale_rows(nc.sync, more_scale_pool, more_scales, (2, 3))
        token_list = load_list(offs, "token_list")
        key_word_pool = load_words(keys_words, T, "key_word_pool")
        load_scale_rows(nc.sync, key_scale_pool, keys_scales, (0, 1))
        note_pool.append(load_plane(notes, 2, "note_pool2"))
        load_scale_rows(nc.sync, key_scale_pool, keys_scales, (2, 3))
        note_pool.append(load_plane(notes, 3, "note_pool3"))
        user_list = load_list(offs4, "user_list")
        user_pool = [load_plane(users2, t, "user_pool%d" % t) for t in range(PACK)]
        val_pool = [load_plane(vals, t, "val_pool%d" % t) for t in range(PACK)]

        def gather_words(pool, index, name):
            picked = tile([P, I], U16, name + "_picked")
            nc.vector.tensor_copy(picked[:], pool[:].indirect(index[:]))
            dealt = tile([P, I], U16, name)
            nc.vector.tensor_copy(out=dealt[:].rearrange("p (t s) -> p s t", t=PACK), in_=picked[:].rearrange("p (s t) -> p s t", t=PACK))
            return dealt

        def gather_scales(pool, index, name):
            dealt = tile([P, I], U8, name)
            nc.vector.tensor_copy(dealt[:].rearrange("p (t s) -> p s t", t=PACK), pool[:].indirect(index[:]))
            return dealt

        def interleave(engine_copy, dst, src):
            engine_copy(out=dst.rearrange("p (c i t) -> p c t i", i=4, t=PACK), in_=src.rearrange("p t (c i) -> p c t i", i=4))

        def quantize(codes, scales, src):
            nc.vector.quantize_mx(out=codes.bitcast(FP8X4), scales=scales, in_=src)

        def weave_pair(engine_copy, dst, src, pair):
            engine_copy(out=dst.rearrange("p (c i t) -> p c t i", i=4, t=PACK)[:, :, 2 * pair : 2 * pair + 2, :], in_=src.rearrange("p u (c i) -> p c u i", i=4))

        more_words_sb = gather_words(more_word_pool, more_list, "more_words_sb")
        more_scales_sb = gather_scales(more_scale_pool, more_list, "more_scales_sb")
        key_words = gather_words(key_word_pool, token_list, "key_words")
        key_scales = gather_scales(key_scale_pool, token_list, "key_scales")

        note_picked = tile([P, PACK, J], BF16, "note_picked")
        for t in range(PACK - 1):
            nc.scalar.activation(note_picked[:, t, :], note_pool[t][:].indirect(note_list[:]), COPY)
        nc.scalar.activation(note_picked[:, PACK - 1, 0:HALF], note_pool[PACK - 1][:].indirect(note_list[:, 0:16]), COPY)
        nc.vector.tensor_copy(note_picked[:, PACK - 1, HALF:J], note_pool[PACK - 1][:].indirect(note_list[:, 16:32]))

        note_woven = tile([P, PACK * J], BF16, "note_woven")
        interleave(nc.vector.tensor_copy, note_woven[:], note_picked[:])
        note_codes = tile([P, J], U32, "note_codes")
        note_scales = tile([P, J], U8, "note_scales")
        quantize(note_codes[:], note_scales[:], note_woven[:])

        table = [bank([P, PACK, CHUNK], c, "table%d" % c) for c in range(J // CHUNK)]

        def table_passes(c, words, word_scales, codes, scales, c0, first):
            for t in range(PACK):
                rows = slice(t * P, (t + 1) * P)
                cols = slice(c0, c0 + CHUNK)
                nc.tensor.matmul_mx(out=table[c][:, t, :], lhsT=words[:, rows].bitcast(FP4X4), lhsT_scale=word_scales[:, rows],
                                    rhs=codes[:, cols].bitcast(FP8X4), rhs_scale=scales[:, cols],
                                    start=(first and t == 0), stop=(not first and t == PACK - 1))

        for c in range(J // CHUNK):
            table_passes(c, key_words, key_scales, note_codes, note_scales, c * CHUNK, True)

        mem_bank = bank([P, PACK, P], 4, "mem_bank")
        for t in range(PACK):
            nc.tensor.transpose(mem_bank[:, t, :], mem_cols[:, t : t + 1].to_broadcast([P, P]), ident[:])

        user_picked = [tile([P, PACK, HALF], BF16, "user_picked%d" % h) for h in range(2)]
        for t in range(PACK):
            for h in range(2):
                window = user_pool[t][:].indirect(user_list[:, 16 * h : 16 * h + 16])
                if t >= 2 and h == 1:
                    nc.vector.tensor_copy(user_picked[h][:, t, :], window)
                else:
                    nc.scalar.activation(user_picked[h][:, t, :], window, COPY)

        mem_rows = tile([P, J], F32, "mem_rows")
        nc.scalar.copy(out=mem_rows[:].rearrange("f (p t) -> f p t", t=PACK), in_=mem_bank[:].rearrange("f t p -> f p t"))

        user_woven = [tile([P, PACK * HALF], BF16, "user_woven%d" % h) for h in range(2)]
        interleave(nc.scalar.copy, user_woven[0][:], user_picked[0][:])
        interleave(nc.vector.tensor_copy, user_woven[1][:], user_picked[1][:])
        for h in (1, 0):
            user_codes = tile([P, HALF], U32, "user_codes%d" % h)
            user_scales = tile([P, HALF], U8, "user_scales%d" % h)
            quantize(user_codes[:], user_scales[:], user_woven[h][:])
            for c in range(2):
                table_passes(2 * h + c, more_words_sb, more_scales_sb, user_codes, user_scales, c * CHUNK, False)

        weight_codes = [tile([P, HALF], U32, "weight_codes%d" % h) for h in range(2)]
        weight_scales = [tile([P, HALF], U8, "weight_scales%d" % h) for h in range(2)]
        weight_woven = [tile([P, PACK * HALF], BF16, "weight_woven%d" % h) for h in range(2)]

        def weigh(c):
            nc.vector.scalar_tensor_tensor(
                out=weight_woven[c // 2][:, c % 2 * CHUNK * PACK : (c % 2 + 1) * CHUNK * PACK].rearrange("p (j t) -> p j t", t=PACK),
                in0=table[c][:].rearrange("p t j -> p j t"), scalar=0.0,
                in1=row_factor[:].unsqueeze(1).to_broadcast([P, CHUNK, PACK]), op0=ALU.max, op1=ALU.mult)

        result_low = tile([P, 2, J], F32, "result_low")
        result_high = [tile([P, 2, HALF], F32, "result_high%d" % h) for h in range(2)]
        out_rows = out_0.rearrange("(p t) j -> p t j", t=PACK)
        halves = [slice(0, HALF), slice(HALF, J)]

        def turn_values(t):
            val_picked = sb.tile([P, I], BF16, name="val_picked%d" % t, tag="val_picked%d" % t, align_bytes=64)
            nc.scalar.activation(val_picked[:], val_pool[t][:].indirect(token_list[:]), COPY)
            pairs = val_picked[:].bitcast(F32)
            turned = bank([P, 2, P], (5, 4, 5, 4)[t], "turned%d" % t)
            for u in range(2):
                nc.tensor.transpose(turned[:, u, :], pairs[:, u : 2 * P : 2], ident[:])
            return turned

        def copy_turned(turned, woven):
            nc.scalar.copy(out=woven.bitcast(F32).rearrange("p (e u) -> p e u", u=2), in_=turned[:].rearrange("p u e -> p e u"))

        def quantize_values(t, woven):
            codes = tile([P, P], U32, "val_codes%d" % t)
            scales = tile([P, P], U8, "val_scales%d" % t)
            quantize(codes[:], scales[:], woven)
            return codes, scales

        def multiply(t, quantized, h):
            sums = bank([P, HALF], ((6, 7), (0, 1), (2, 3), (6, 7))[t][h], "sums%d_%d" % (t, h))
            nc.tensor.matmul_mx(out=sums[:], lhsT=quantized[0][:].bitcast(FP8X4), lhsT_scale=quantized[1][:],
                                rhs=weight_codes[h][:].bitcast(FP8X4), rhs_scale=weight_scales[h][:], start=True, stop=True)
            return sums


        def carry(t, sums, h):
            first, last = h * HALF + 1, min((h + 1) * HALF + 1, J)
            nc.vector.tensor_tensor(carried[t][:, first:last], sums[:, 0 : last - first], mem_rows[:, first:last], ALU.mult)

        def result_rows(t, h):
            return result_low[:, t, halves[h]] if t < 2 else result_high[h][:, t - 2, :]

        def subtract(t, sums, h):
            nc.vector.tensor_tensor(result_rows(t, h), sums[:], carried[t][:, halves[h]], ALU.subtract)

        def woven_in_pool_slot(t):
            return sb.tile([P, PACK * P], BF16, name="val_woven%d" % t, tag="val_pool%d" % (t + 1), align_bytes=64)[:]

        def finish_values(t, turned, woven):
            copy_turned(turned, woven)
            return quantize_values(t, woven)

        for c in (2, 3, 0):
            weigh(c)
        quantize(weight_codes[1][:], weight_scales[1][:], weight_woven[1][:])
        turned = [turn_values(0)]
        quantized = [finish_values(0, turned[0], tile([P, PACK * P], BF16, "val_woven0")[:])]
        turned.append(turn_values(1))
        weigh(1)
        quantize(weight_codes[0][:], weight_scales[0][:], weight_woven[0][:])
        for t in range(PACK):
            order = (1, 0) if t == 0 else (0, 1)
            sums = {h: multiply(t, quantized[t], h) for h in order}
            carry(t, sums[order[0]], order[0])
            if t == 1:
                quantized.append(finish_values(2, turned[2], carried[1][:, HALF + 16 : J + 16].bitcast(BF16)))
            carry(t, sums[order[1]], order[1])
            if t == 0:
                turned.append(turn_values(2))
                quantized.append(finish_values(1, turned[1], woven_in_pool_slot(1)))
            if t == 2:
                quantized.append(finish_values(3, turn_values(3), result_rows(2, 0).bitcast(BF16)))
            for h in range(2):
                subtract(t, sums[h], h)
            if t == 1:
                nc.sync.dma_start(out=out_rows[:, 0:2, :], in_=result_low[:])
        for h in range(2):
            nc.sync.dma_start(out=out_rows[:, 2:4, halves[h]], in_=result_high[h][:])
        out_codes = tile([P, J], U32, "out_codes")
        out_scales = tile([P, J], U8, "out_scales")
        out_words = out_1[0].rearrange("p c r -> p (c r)").bitcast(I32)
        result_woven = [sb.tile([P, PACK * HALF], BF16, name="result_woven%d" % h, tag=tag, align_bytes=64)
                        for h, tag in enumerate(("val_picked3", "ident"))]
        for h in range(2):
            weave_pair(nc.scalar.copy, result_woven[h][:], result_low[:, :, halves[h]], 0)
        for h in range(2):
            weave_pair(nc.vector.tensor_copy, result_woven[h][:], result_high[h][:], 1)
        for h in range(2):
            quantize(out_codes[:, halves[h]], out_scales[:, halves[h]], result_woven[h][:])
            nc.sync.dma_start(out=out_words[:, halves[h]], in_=out_codes[:, halves[h]].bitcast(I32))
        for q in range(4):
            queue = nc.sync if q % 2 == 0 else nc.scalar
            queue.dma_start(out=out_2[0, q:16:4, :].bitcast(I32), in_=out_scales[q:P:32, :].bitcast(I32))
